import numpy as np
CORES = [66,74,82,90,194,202,210,218]
N = 8
R, T = 256, 512
def entries(a): return a.T.reshape(-1)
def pack(v, P): return np.ascontiguousarray(np.asarray(v, np.int32).reshape(-1, P).T)
def lists(rng, how):
    I = rng.integers(0, N * R, (N, T))
    if how == "alike": I[:] = rng.integers(0, N * R, (N, 1))
    if how == "distinct": I = np.stack([rng.permutation(N * R)[:T] for r in range(N)])
    if how == "hotrank": I = R * int(rng.integers(N)) + rng.integers(0, R, (N, T))
    if how == "own": I = R * np.arange(N).reshape(N, 1) + rng.integers(0, R, (N, T))
    if how == "edge": I = R * rng.integers(0, N, (N, T)) + np.where(rng.random((N, T)) < 0.5, 0, R - 1)
    return {"idx": np.stack([pack(I[r], 16) for r in range(N)])}
def setup_inputs(rng):
    return dict({"tab": rng.standard_normal((N, 128, R), dtype=np.float32)}, **lists(rng, "uniform"))
def setup_inputs_alike(rng):
    d = setup_inputs(rng); d.update(lists(rng, "alike"))
    for k in ("tab",): d[k] = (d[k].astype(np.float32) * 1048576.0).astype(d[k].dtype)
    return d
def setup_inputs_distinct(rng):
    d = setup_inputs(rng); d.update(lists(rng, "distinct"))
    for k in ("tab",): d[k] = (d[k].astype(np.float32) * (1 / 1024.0)).astype(d[k].dtype)
    return d
def setup_inputs_edge(rng):
    d = setup_inputs(rng); d.update(lists(rng, "edge"))
    return d
def setup_inputs_hotrank(rng):
    d = setup_inputs(rng); d.update(lists(rng, "hotrank"))
    return d
def setup_inputs_own(rng):
    d = setup_inputs(rng); d.update(lists(rng, "own"))
    return d
def check_inputs(x):
    bad = []
    if x["idx"].min() < 0 or x["idx"].max() >= N * R: bad.append("idx out of range")
    return bad
def reference(tab, idx):
    A = np.concatenate(list(tab), axis=1)
    return {"y": np.stack([A[:, entries(idx[r])] for r in range(N)])}

@@ -1,0 +1,55 @@
+from concourse.bass import DstId, RemoteDMATransfer
+
+N, R, L = 8, 256, 512
+
+SCRATCH = {
+    "win": ("sbuf", [128, N * R], "float32"),
+    "res": ("sbuf", [128, L], "float32"),
+    "ix32": ("sbuf", [128, L // 16], "int32"),
+    "off": ("sbuf", [128, L // 16], "uint16"),
+}
+SEMAPHORES = ["ld", "ix", "cv", "arr", "sent", "ga", "gb", "st"]
+
+
+def _bits(m):
+    return bin(m).count("1")
+
+
+def rank_program(g, core, T, topo):
+    rank = T.rank_of(core)
+    if rank is None:
+        return
+    S = T.sem
+    own = T.win[:, R * rank:R * (rank + 1)]
+
+    g.sync.dma_start(own, T.tab[:, :]).then_inc(S.ld, 16)
+    for k in range(8):
+        g.scalar.dma_start(T.ix32[16 * k:16 * k + 16, :], T.idx[:, :]).then_inc(S.ix, 16)
+
+    g.vector.wait_ge(S.ix, 16 * 8)
+    g.vector.tensor_copy(T.off[:, :], T.ix32[:, :]).then_inc(S.cv, 1)
+
+    others = [d for d in T.cores if d != core]
+    mask = topo.mask(core, others[0])
+    for d in others:
+        mask &= topo.mask(core, d)
+    ids = []
+    for d in others:
+        rid, pid = topo.addr(d, core)
+        ids.append(DstId(rid=rid, pnc=pid))
+    g.wait_ge(S.ld, 16)
+    g.remote_dma_fused([RemoteDMATransfer(dst_ids=ids, dma_engine_mask=mask, remote_sem=S.arr,
+                                          srcs=[own], dsts=[own] * len(others), alu_op=0)], local_sem=S.sent)
+
+    h = L // 2
+    g.vector.wait_ge(S.cv, 1)
+    g.vector.wait_ge(S.ld, 16)
+    g.vector.wait_ge(S.arr, _bits(mask) * len(others))
+    g.vector.tensor_copy(T.res[:, 0:h], T.win[:, :].indirect(T.off[:, 0:h // 16])).then_inc(S.ga, 1)
+    g.vector.tensor_copy(T.res[:, h:L], T.win[:, :].indirect(T.off[:, h // 16:L // 16])).then_inc(S.gb, 1)
+    g.sync.wait_ge(S.ga, 1)
+    g.sync.dma_start(T.y[:, 0:h], T.res[:, 0:h]).then_inc(S.st, 16)
+    g.scalar.wait_ge(S.gb, 1)
+    g.scalar.dma_start(T.y[:, h:L], T.res[:, h:L]).then_inc(S.st, 16)
+    g.wait_ge(S.sent, _bits(mask))
+    g.wait_ge(S.st, 32)

@@ -1,6 +1,7 @@
 from concourse.bass import DstId, RemoteDMATransfer
 
 N, R, L = 8, 256, 512
+WORLD = 256
 
 SCRATCH = {
     "win": ("sbuf", [128, N * R], "float32"),
@@ -8,19 +9,57 @@ SCRATCH = {
     "ix32": ("sbuf", [128, L // 16], "int32"),
     "off": ("sbuf", [128, L // 16], "uint16"),
 }
-SEMAPHORES = ["ld", "ix", "cv", "arr", "sent", "ga", "gb", "st"]
+SEMAPHORES = ["ld", "ix", "cv", "arr", "got", "sent", "ga", "gb", "st"]
 
 
 def _bits(m):
     return bin(m).count("1")
 
 
+def _plan(T, topo, rc):
+    others = [d for d in T.cores if d != rc]
+    chipmates = [c for c in range(WORLD)
+                 if c != rc and topo.host(c) == topo.host(rc) and topo.chip(c) == topo.chip(rc)]
+    full = [c for c in chipmates if all(topo.may_write(c, d) for d in others)]
+    near = [c for c in full if topo.die(c) == topo.die(rc)][:1]
+    far = [c for c in full if topo.die(c) != topo.die(rc)][:2]
+    k = others.index([d for d in others if topo.mates(rc, d)][0])
+    order = others[k:] + others[:k]
+    return [(rc, 0, order[0:4]), (near[0], 0, order[4:7]), (far[0], 1, order[0:4]), (far[1], 1, order[4:7])]
+
+
+def _send(g, T, topo, core, ap, dests, mask):
+    ids = []
+    for d in dests:
+        rid, pid = topo.addr(d, core)
+        ids.append(DstId(rid=rid, pnc=pid))
+    return RemoteDMATransfer(dst_ids=ids, dma_engine_mask=mask, remote_sem=T.sem.arr,
+                             srcs=[ap], dsts=[ap] * len(dests), alu_op=0)
+
+
 def rank_program(g, core, T, topo):
-    rank = T.rank_of(core)
-    if rank is None:
-        return
     S = T.sem
+    rank = T.rank_of(core)
+    hw = R // 2
+
+    if rank is None:
+        for r, rc in enumerate(T.cores):
+            if topo.host(rc) != topo.host(core) or topo.chip(rc) != topo.chip(core):
+                continue
+            for (c, half, dests) in _plan(T, topo, rc)[1:]:
+                if c != core:
+                    continue
+                ap = T.win[:, R * r + hw * half:R * r + hw * (half + 1)]
+                off = topo.mask(core, dests[0])
+                for d in dests:
+                    off &= topo.mask(core, d)
+                g.wait_ge(S.got, _bits(topo.mask(rc, core)) // 2)
+                g.remote_dma_fused([_send(g, T, topo, core, ap, dests, off)], local_sem=S.sent)
+                g.wait_ge(S.sent, _bits(off))
+        return
+
     own = T.win[:, R * rank:R * (rank + 1)]
+    halves = [T.win[:, R * rank + hw * h:R * rank + hw * (h + 1)] for h in range(2)]
 
     g.sync.dma_start(own, T.tab[:, :]).then_inc(S.ld, 16)
     for k in range(8):
@@ -29,27 +68,34 @@ def rank_program(g, core, T, topo):
     g.vector.wait_ge(S.ix, 16 * 8)
     g.vector.tensor_copy(T.off[:, :], T.ix32[:, :]).then_inc(S.cv, 1)
 
-    others = [d for d in T.cores if d != core]
-    mask = topo.mask(core, others[0])
-    for d in others:
-        mask &= topo.mask(core, d)
-    ids = []
-    for d in others:
-        rid, pid = topo.addr(d, core)
-        ids.append(DstId(rid=rid, pnc=pid))
+    plan = _plan(T, topo, core)
+    off = topo.mask(core, plan[0][2][0])
+    for d in T.cores:
+        if d != core:
+            off &= topo.mask(core, d)
+    on = topo.mask(core, plan[1][0])
+    hi = on & ~off
     g.wait_ge(S.ld, 16)
-    g.remote_dma_fused([RemoteDMATransfer(dst_ids=ids, dma_engine_mask=mask, remote_sem=S.arr,
-                                          srcs=[own], dsts=[own] * len(others), alu_op=0)], local_sem=S.sent)
+    hand = []
+    for (mask, half, cs) in ((hi, 1, [plan[2][0], plan[3][0]]), (on & ~hi, 0, [plan[1][0]])):
+        ids = []
+        for c in cs:
+            rid, pid = topo.addr(c, core)
+            ids.append(DstId(rid=rid, pnc=pid))
+        hand.append(RemoteDMATransfer(dst_ids=ids, dma_engine_mask=mask, remote_sem=S.got,
+                                      srcs=[halves[half]], dsts=[halves[half]] * len(cs), alu_op=0))
+    g.remote_dma_fused(hand, local_sem=S.sent)
+    g.remote_dma_fused([_send(g, T, topo, core, halves[0], plan[0][2], off)], local_sem=S.sent)
 
     h = L // 2
     g.vector.wait_ge(S.cv, 1)
     g.vector.wait_ge(S.ld, 16)
-    g.vector.wait_ge(S.arr, _bits(mask) * len(others))
+    g.vector.wait_ge(S.arr, _bits(off) * 2 * (N - 1))
     g.vector.tensor_copy(T.res[:, 0:h], T.win[:, :].indirect(T.off[:, 0:h // 16])).then_inc(S.ga, 1)
     g.vector.tensor_copy(T.res[:, h:L], T.win[:, :].indirect(T.off[:, h // 16:L // 16])).then_inc(S.gb, 1)
     g.sync.wait_ge(S.ga, 1)
     g.sync.dma_start(T.y[:, 0:h], T.res[:, 0:h]).then_inc(S.st, 16)
     g.scalar.wait_ge(S.gb, 1)
     g.scalar.dma_start(T.y[:, h:L], T.res[:, h:L]).then_inc(S.st, 16)
-    g.wait_ge(S.sent, _bits(mask))
+    g.wait_ge(S.sent, _bits(on) + _bits(off))
     g.wait_ge(S.st, 32)

@@ -1,7 +1,9 @@
 from concourse.bass import DstId, RemoteDMATransfer
+from concourse.mybir import ActivationFunctionType
 
 N, R, L = 8, 256, 512
 WORLD = 256
+QW = R // 4
 
 SCRATCH = {
     "win": ("sbuf", [128, N * R], "float32"),
@@ -9,93 +11,116 @@ SCRATCH = {
     "ix32": ("sbuf", [128, L // 16], "int32"),
     "off": ("sbuf", [128, L // 16], "uint16"),
 }
-SEMAPHORES = ["ld", "ix", "cv", "arr", "got", "sent", "ga", "gb", "st"]
+SEMAPHORES = ["ld0", "ld1", "ix", "cv", "arr", "got", "sent", "ga", "gb", "st"]
 
 
 def _bits(m):
     return bin(m).count("1")
 
 
+def _split(m):
+    b = [1 << i for i in range(m.bit_length()) if (m >> i) & 1]
+    return sum(b[:len(b) // 2]), sum(b[len(b) // 2:])
+
+
 def _plan(T, topo, rc):
     others = [d for d in T.cores if d != rc]
-    chipmates = [c for c in range(WORLD)
-                 if c != rc and topo.host(c) == topo.host(rc) and topo.chip(c) == topo.chip(rc)]
-    full = [c for c in chipmates if all(topo.may_write(c, d) for d in others)]
-    near = [c for c in full if topo.die(c) == topo.die(rc)][:1]
-    far = [c for c in full if topo.die(c) != topo.die(rc)][:2]
-    k = others.index([d for d in others if topo.mates(rc, d)][0])
-    order = others[k:] + others[:k]
-    return [(rc, 0, order[0:4]), (near[0], 0, order[4:7]), (far[0], 1, order[0:4]), (far[1], 1, order[4:7])]
+    grp = [d for d in T.cores if d == rc or topo.same_plane(rc, d)]
+    pos = grp.index(rc)
+    plane = [grp[(pos + k) % len(grp)] for k in range(1, len(grp))]
+    cross = [d for d in others if d not in plane]
+    cross = cross[pos:] + cross[:pos]
+    chip = [c for c in range(WORLD)
+            if c != rc and topo.host(c) == topo.host(rc) and topo.chip(c) == topo.chip(rc)]
+    own = [c for c in chip if all(topo.may_write(c, d) for d in cross)]
+    rest = [c for c in chip if c not in own and all(topo.may_write(c, d) for d in plane)]
+    near = [[c for c in cs if topo.die(c) == topo.die(rc)] for cs in (own, rest)]
+    far = [[c for c in cs if topo.die(c) != topo.die(rc)] for cs in (own, rest)]
+    return {"R": (rc, 0, cross), "N": (near[0][0], 1, cross), "F0": (far[0][0], 2, cross), "F1": (far[0][1], 3, cross),
+            "Pa": (near[1][0], 0, plane), "Pb": (near[1][1], 1, plane),
+            "Pc": (far[1][0], 2, plane), "Pd": (far[1][1], 3, plane)}
 
 
-def _send(g, T, topo, core, ap, dests, mask):
+def _xfer(topo, core, ap, dests, sem, mask):
     ids = []
     for d in dests:
         rid, pid = topo.addr(d, core)
         ids.append(DstId(rid=rid, pnc=pid))
-    return RemoteDMATransfer(dst_ids=ids, dma_engine_mask=mask, remote_sem=T.sem.arr,
+    return RemoteDMATransfer(dst_ids=ids, dma_engine_mask=mask, remote_sem=sem,
                              srcs=[ap], dsts=[ap] * len(dests), alu_op=0)
+
+
+def _masks(topo, rc, plan):
+    off = topo.mask(rc, plan["R"][2][0])
+    for d in plan["R"][2]:
+        off &= topo.mask(rc, d)
+    return off, topo.mask(rc, plan["N"][0]) & ~off
+
+
+def _hands(topo, rc, plan):
+    off, hi = _masks(topo, rc, plan)
+    ha, hb = _split(hi)
+    la, lb = _split(off)
+    return [[("F0", ha), ("F1", hb)], [("Pc", ha), ("Pd", hb)]], [[("N", la), ("Pb", lb)], [("Pa", off)]]
 
 
 def rank_program(g, core, T, topo):
     S = T.sem
-    rank = T.rank_of(core)
-    hw = R // 2
+    home = [rc for rc in T.cores if topo.host(rc) == topo.host(core) and topo.chip(rc) == topo.chip(core)]
+    if not home:
+        return
+    rc = home[0]
+    r = T.rank_of(rc)
+    plan = _plan(T, topo, rc)
+    role = [k for k in plan if plan[k][0] == core]
+    if not role:
+        return
+    role = role[0]
+    quarter = [T.win[:, R * r + QW * q:R * r + QW * (q + 1)] for q in range(4)]
+    far_calls, near_calls = _hands(topo, rc, plan)
+    dests = plan[role][2]
+    out = topo.mask(core, dests[0])
+    for d in dests:
+        out &= topo.mask(core, d)
 
-    if rank is None:
-        for r, rc in enumerate(T.cores):
-            if topo.host(rc) != topo.host(core) or topo.chip(rc) != topo.chip(core):
-                continue
-            for (c, half, dests) in _plan(T, topo, rc)[1:]:
-                if c != core:
-                    continue
-                ap = T.win[:, R * r + hw * half:R * r + hw * (half + 1)]
-                off = topo.mask(core, dests[0])
-                for d in dests:
-                    off &= topo.mask(core, d)
-                g.wait_ge(S.got, _bits(topo.mask(rc, core)) // 2)
-                g.remote_dma_fused([_send(g, T, topo, core, ap, dests, off)], local_sem=S.sent)
-                g.wait_ge(S.sent, _bits(off))
+    if role != "R":
+        n = [_bits(m) for call in far_calls + near_calls for (k, m) in call if k == role][0]
+        g.wait_ge(S.got, n)
+        g.remote_dma_fused([_xfer(topo, core, quarter[plan[role][1]], dests, S.arr, out)], local_sem=S.sent)
+        g.wait_ge(S.sent, _bits(out))
         return
 
-    own = T.win[:, R * rank:R * (rank + 1)]
-    halves = [T.win[:, R * rank + hw * h:R * rank + hw * (h + 1)] for h in range(2)]
-
-    g.sync.dma_start(own, T.tab[:, :]).then_inc(S.ld, 16)
+    hw = R // 2
+    g.sync.dma_start(T.win[:, R * r + hw:R * (r + 1)], T.tab[:, hw:R]).then_inc(S.ld1, 16)
+    g.scalar.dma_start(T.win[:, R * r:R * r + hw], T.tab[:, 0:hw]).then_inc(S.ld0, 16)
     for k in range(8):
         g.scalar.dma_start(T.ix32[16 * k:16 * k + 16, :], T.idx[:, :]).then_inc(S.ix, 16)
 
     g.vector.wait_ge(S.ix, 16 * 8)
     g.vector.tensor_copy(T.off[:, :], T.ix32[:, :]).then_inc(S.cv, 1)
 
-    plan = _plan(T, topo, core)
-    off = topo.mask(core, plan[0][2][0])
-    for d in T.cores:
-        if d != core:
-            off &= topo.mask(core, d)
-    on = topo.mask(core, plan[1][0])
-    hi = on & ~off
-    g.wait_ge(S.ld, 16)
-    hand = []
-    for (mask, half, cs) in ((hi, 1, [plan[2][0], plan[3][0]]), (on & ~hi, 0, [plan[1][0]])):
-        ids = []
-        for c in cs:
-            rid, pid = topo.addr(c, core)
-            ids.append(DstId(rid=rid, pnc=pid))
-        hand.append(RemoteDMATransfer(dst_ids=ids, dma_engine_mask=mask, remote_sem=S.got,
-                                      srcs=[halves[half]], dsts=[halves[half]] * len(cs), alu_op=0))
-    g.remote_dma_fused(hand, local_sem=S.sent)
-    g.remote_dma_fused([_send(g, T, topo, core, halves[0], plan[0][2], off)], local_sem=S.sent)
+    sent = 0
+    for (sem, calls) in ((S.ld1, far_calls), (S.ld0, near_calls)):
+        g.wait_ge(sem, 16)
+        for call in calls:
+            g.remote_dma_fused([_xfer(topo, core, quarter[plan[k][1]], [plan[k][0]], S.got, m) for (k, m) in call],
+                               local_sem=S.sent)
+            sent += sum(_bits(m) for (k, m) in call)
+    g.remote_dma_fused([_xfer(topo, core, quarter[0], dests, S.arr, out)], local_sem=S.sent)
+    sent += _bits(out)
 
-    h = L // 2
-    g.vector.wait_ge(S.cv, 1)
-    g.vector.wait_ge(S.ld, 16)
-    g.vector.wait_ge(S.arr, _bits(off) * 2 * (N - 1))
-    g.vector.tensor_copy(T.res[:, 0:h], T.win[:, :].indirect(T.off[:, 0:h // 16])).then_inc(S.ga, 1)
-    g.vector.tensor_copy(T.res[:, h:L], T.win[:, :].indirect(T.off[:, h // 16:L // 16])).then_inc(S.gb, 1)
+    h2 = L // 2
+    for q in (g.vector, g.scalar):
+        q.wait_ge(S.cv, 1)
+        q.wait_ge(S.ld0, 16)
+        q.wait_ge(S.ld1, 16)
+        q.wait_ge(S.arr, _bits(out) * 4 * (N - 1))
+    g.vector.tensor_copy(T.res[:, 0:h2], T.win[:, :].indirect(T.off[:, 0:h2 // 16])).then_inc(S.ga, 1)
+    g.scalar.activation(T.res[:, h2:L], T.win[:, :].indirect(T.off[:, h2 // 16:L // 16]),
+                        ActivationFunctionType.Copy).then_inc(S.gb, 1)
     g.sync.wait_ge(S.ga, 1)
-    g.sync.dma_start(T.y[:, 0:h], T.res[:, 0:h]).then_inc(S.st, 16)
+    g.sync.dma_start(T.y[:, 0:h2], T.res[:, 0:h2]).then_inc(S.st, 16)
     g.scalar.wait_ge(S.gb, 1)
-    g.scalar.dma_start(T.y[:, h:L], T.res[:, h:L]).then_inc(S.st, 16)
-    g.wait_ge(S.sent, _bits(on) + _bits(off))
+    g.scalar.dma_start(T.y[:, h2:L], T.res[:, h2:L]).then_inc(S.st, 16)
+    g.wait_ge(S.sent, sent)
     g.wait_ge(S.st, 32)

@@ -11,7 +11,7 @@ SCRATCH = {
     "ix32": ("sbuf", [128, L // 16], "int32"),
     "off": ("sbuf", [128, L // 16], "uint16"),
 }
-SEMAPHORES = ["ld0", "ld1", "ix", "cv", "arr", "got", "sent", "ga", "gb", "st"]
+SEMAPHORES = ["ld0", "ld1", "ix", "cv", "arr", "lq", "got", "sent", "ga", "gb", "st"]
 
 
 def _bits(m):
@@ -30,15 +30,16 @@ def _plan(T, topo, rc):
     plane = [grp[(pos + k) % len(grp)] for k in range(1, len(grp))]
     cross = [d for d in others if d not in plane]
     cross = cross[pos:] + cross[:pos]
+    mate = [d for d in cross if topo.mates(rc, d)]
     chip = [c for c in range(WORLD)
             if c != rc and topo.host(c) == topo.host(rc) and topo.chip(c) == topo.chip(rc)]
     own = [c for c in chip if all(topo.may_write(c, d) for d in cross)]
     rest = [c for c in chip if c not in own and all(topo.may_write(c, d) for d in plane)]
     near = [[c for c in cs if topo.die(c) == topo.die(rc)] for cs in (own, rest)]
     far = [[c for c in cs if topo.die(c) != topo.die(rc)] for cs in (own, rest)]
-    return {"R": (rc, 0, cross), "N": (near[0][0], 1, cross), "F0": (far[0][0], 2, cross), "F1": (far[0][1], 3, cross),
-            "Pa": (near[1][0], 0, plane), "Pb": (near[1][1], 1, plane),
-            "Pc": (far[1][0], 2, plane), "Pd": (far[1][1], 3, plane)}
+    return {"R": (rc, 0, plane + mate), "N": (near[0][0], 1, cross), "Pa": (near[1][0], 1, plane),
+            "F0": (far[0][0], 2, cross), "Pb": (near[1][1], 2, plane),
+            "F1": (far[0][1], 3, cross), "Pd": (far[1][0], 3, plane)}
 
 
 def _xfer(topo, core, ap, dests, sem, mask):
@@ -50,18 +51,14 @@ def _xfer(topo, core, ap, dests, sem, mask):
                              srcs=[ap], dsts=[ap] * len(dests), alu_op=0)
 
 
-def _masks(topo, rc, plan):
+def _hands(topo, rc, plan):
     off = topo.mask(rc, plan["R"][2][0])
     for d in plan["R"][2]:
         off &= topo.mask(rc, d)
-    return off, topo.mask(rc, plan["N"][0]) & ~off
-
-
-def _hands(topo, rc, plan):
-    off, hi = _masks(topo, rc, plan)
+    hi = topo.mask(rc, plan["N"][0]) & ~off
     ha, hb = _split(hi)
     la, lb = _split(off)
-    return [[("F0", ha), ("F1", hb)], [("Pc", ha), ("Pd", hb)]], [[("N", la), ("Pb", lb)], [("Pa", off)]]
+    return [(1, [("F0", ha), ("F1", hb)]), (0, [("N", la), ("Pa", lb)]), (1, [("Pd", ha), ("Pb", hb)])]
 
 
 def rank_program(g, core, T, topo):
@@ -77,14 +74,14 @@ def rank_program(g, core, T, topo):
         return
     role = role[0]
     quarter = [T.win[:, R * r + QW * q:R * r + QW * (q + 1)] for q in range(4)]
-    far_calls, near_calls = _hands(topo, rc, plan)
+    hands = _hands(topo, rc, plan)
     dests = plan[role][2]
     out = topo.mask(core, dests[0])
     for d in dests:
         out &= topo.mask(core, d)
 
     if role != "R":
-        n = [_bits(m) for call in far_calls + near_calls for (k, m) in call if k == role][0]
+        n = [_bits(m) for (h, call) in hands for (k, m) in call if k == role][0]
         g.wait_ge(S.got, n)
         g.remote_dma_fused([_xfer(topo, core, quarter[plan[role][1]], dests, S.arr, out)], local_sem=S.sent)
         g.wait_ge(S.sent, _bits(out))
@@ -100,21 +97,28 @@ def rank_program(g, core, T, topo):
     g.vector.tensor_copy(T.off[:, :], T.ix32[:, :]).then_inc(S.cv, 1)
 
     sent = 0
-    for (sem, calls) in ((S.ld1, far_calls), (S.ld0, near_calls)):
-        g.wait_ge(sem, 16)
-        for call in calls:
-            g.remote_dma_fused([_xfer(topo, core, quarter[plan[k][1]], [plan[k][0]], S.got, m) for (k, m) in call],
-                               local_sem=S.sent)
-            sent += sum(_bits(m) for (k, m) in call)
-    g.remote_dma_fused([_xfer(topo, core, quarter[0], dests, S.arr, out)], local_sem=S.sent)
-    sent += _bits(out)
+    for (h, call) in hands:
+        g.wait_ge((S.ld0, S.ld1)[h], 16)
+        g.remote_dma_fused([_xfer(topo, core, quarter[plan[k][1]], [plan[k][0]], S.got, m) for (k, m) in call],
+                           local_sem=S.sent)
+        sent += sum(_bits(m) for (k, m) in call)
+    plane, mate = dests[:-1], dests[-1:]
+    nb = _bits(out)
+    g.remote_dma_fused([_xfer(topo, core, quarter[0], plane, S.lq, out)], local_sem=S.sent)
+    g.remote_dma_fused([_xfer(topo, core, quarter[0], mate, S.arr, out)], local_sem=S.sent)
+    g.wait_ge(S.lq, nb * len(plane))
+    for s in plane:
+        ap = T.win[:, R * T.rank_of(s):R * T.rank_of(s) + QW]
+        g.remote_dma_fused([_xfer(topo, core, ap, mate, S.arr, out)], local_sem=S.sent)
+    sent += nb * (2 + len(plane))
 
     h2 = L // 2
     for q in (g.vector, g.scalar):
         q.wait_ge(S.cv, 1)
         q.wait_ge(S.ld0, 16)
         q.wait_ge(S.ld1, 16)
-        q.wait_ge(S.arr, _bits(out) * 4 * (N - 1))
+        q.wait_ge(S.lq, nb * len(plane))
+        q.wait_ge(S.arr, nb * (4 * (N - 1) - len(plane)))
     g.vector.tensor_copy(T.res[:, 0:h2], T.win[:, :].indirect(T.off[:, 0:h2 // 16])).then_inc(S.ga, 1)
     g.scalar.activation(T.res[:, h2:L], T.win[:, :].indirect(T.off[:, h2 // 16:L // 16]),
                         ActivationFunctionType.Copy).then_inc(S.gb, 1)

from concourse.bass import DstId, RemoteDMATransfer
from concourse.mybir import ActivationFunctionType

N, R, L = 8, 256, 512
WORLD = 256
QW = R // 4

SCRATCH = {
    "win": ("sbuf", [128, N * R], "float32"),
    "res": ("sbuf", [128, L], "float32"),
    "ix32": ("sbuf", [128, L // 16], "int32"),
    "off": ("sbuf", [128, L // 16], "uint16"),
}
SEMAPHORES = ["ld0", "ld1", "ix", "cv", "arr", "lq", "got", "sent", "ga", "gb", "st"]


def _bits(m):
    return bin(m).count("1")


def _split(m):
    b = [1 << i for i in range(m.bit_length()) if (m >> i) & 1]
    return sum(b[:len(b) // 2]), sum(b[len(b) // 2:])


def _plan(T, topo, rc):
    others = [d for d in T.cores if d != rc]
    grp = [d for d in T.cores if d == rc or topo.same_plane(rc, d)]
    pos = grp.index(rc)
    plane = [grp[(pos + k) % len(grp)] for k in range(1, len(grp))]
    cross = [d for d in others if d not in plane]
    cross = cross[pos:] + cross[:pos]
    mate = [d for d in cross if topo.mates(rc, d)]
    chip = [c for c in range(WORLD)
            if c != rc and topo.host(c) == topo.host(rc) and topo.chip(c) == topo.chip(rc)]
    own = [c for c in chip if all(topo.may_write(c, d) for d in cross)]
    rest = [c for c in chip if c not in own and all(topo.may_write(c, d) for d in plane)]
    near = [[c for c in cs if topo.die(c) == topo.die(rc)] for cs in (own, rest)]
    far = [[c for c in cs if topo.die(c) != topo.die(rc)] for cs in (own, rest)]
    return {"R": (rc, 0, plane + mate), "N": (near[0][0], 1, cross), "Pa": (near[1][0], 1, plane),
            "F0": (far[0][0], 2, cross), "Pb": (near[1][1], 2, plane),
            "F1": (far[0][1], 3, cross), "Pd": (far[1][0], 3, plane)}


def _xfer(topo, core, ap, dests, sem, mask):
    ids = []
    for d in dests:
        rid, pid = topo.addr(d, core)
        ids.append(DstId(rid=rid, pnc=pid))
    return RemoteDMATransfer(dst_ids=ids, dma_engine_mask=mask, remote_sem=sem,
                             srcs=[ap], dsts=[ap] * len(dests), alu_op=0)


def _hands(topo, rc, plan):
    off = topo.mask(rc, plan["R"][2][0])
    for d in plan["R"][2]:
        off &= topo.mask(rc, d)
    hi = topo.mask(rc, plan["N"][0]) & ~off
    ha, hb = _split(hi)
    la, lb = _split(off)
    return [(1, [("F0", ha), ("F1", hb)]), (0, [("N", la), ("Pa", lb)]), (1, [("Pd", ha), ("Pb", hb)])]


def rank_program(g, core, T, topo):
    S = T.sem
    home = [rc for rc in T.cores if topo.host(rc) == topo.host(core) and topo.chip(rc) == topo.chip(core)]
    if not home:
        return
    rc = home[0]
    r = T.rank_of(rc)
    plan = _plan(T, topo, rc)
    role = [k for k in plan if plan[k][0] == core]
    if not role:
        return
    role = role[0]
    quarter = [T.win[:, R * r + QW * q:R * r + QW * (q + 1)] for q in range(4)]
    hands = _hands(topo, rc, plan)
    dests = plan[role][2]
    out = topo.mask(core, dests[0])
    for d in dests:
        out &= topo.mask(core, d)

    if role != "R":
        n = [_bits(m) for (h, call) in hands for (k, m) in call if k == role][0]
        g.wait_ge(S.got, n)
        g.remote_dma_fused([_xfer(topo, core, quarter[plan[role][1]], dests, S.arr, out)], local_sem=S.sent)
        g.wait_ge(S.sent, _bits(out))
        return

    hw = R // 2
    g.sync.dma_start(T.win[:, R * r + hw:R * (r + 1)], T.tab[:, hw:R]).then_inc(S.ld1, 16)
    g.scalar.dma_start(T.win[:, R * r:R * r + hw], T.tab[:, 0:hw]).then_inc(S.ld0, 16)
    for k in range(8):
        g.scalar.dma_start(T.ix32[16 * k:16 * k + 16, :], T.idx[:, :]).then_inc(S.ix, 16)

    g.vector.wait_ge(S.ix, 16 * 8)
    g.vector.tensor_copy(T.off[:, :], T.ix32[:, :]).then_inc(S.cv, 1)

    sent = 0
    for (h, call) in hands:
        g.wait_ge((S.ld0, S.ld1)[h], 16)
        g.remote_dma_fused([_xfer(topo, core, quarter[plan[k][1]], [plan[k][0]], S.got, m) for (k, m) in call],
                           local_sem=S.sent)
        sent += sum(_bits(m) for (k, m) in call)
    plane, mate = dests[:-1], dests[-1:]
    nb = _bits(out)
    g.remote_dma_fused([_xfer(topo, core, quarter[0], plane, S.lq, out)], local_sem=S.sent)
    g.remote_dma_fused([_xfer(topo, core, quarter[0], mate, S.arr, out)], local_sem=S.sent)
    g.wait_ge(S.lq, nb * len(plane))
    for s in plane:
        ap = T.win[:, R * T.rank_of(s):R * T.rank_of(s) + QW]
        g.remote_dma_fused([_xfer(topo, core, ap, mate, S.arr, out)], local_sem=S.sent)
    sent += nb * (2 + len(plane))

    h2 = L // 2
    for q in (g.vector, g.scalar):
        q.wait_ge(S.cv, 1)
        q.wait_ge(S.ld0, 16)
        q.wait_ge(S.ld1, 16)
        q.wait_ge(S.lq, nb * len(plane))
        q.wait_ge(S.arr, nb * (4 * (N - 1) - len(plane)))
    g.vector.tensor_copy(T.res[:, 0:h2], T.win[:, :].indirect(T.off[:, 0:h2 // 16])).then_inc(S.ga, 1)
    g.scalar.activation(T.res[:, h2:L], T.win[:, :].indirect(T.off[:, h2 // 16:L // 16]),
                        ActivationFunctionType.Copy).then_inc(S.gb, 1)
    g.sync.wait_ge(S.ga, 1)
    g.sync.dma_start(T.y[:, 0:h2], T.res[:, 0:h2]).then_inc(S.st, 16)
    g.scalar.wait_ge(S.gb, 1)
    g.scalar.dma_start(T.y[:, h2:L], T.res[:, h2:L]).then_inc(S.st, 16)
    g.wait_ge(S.sent, sent)
    g.wait_ge(S.st, 32)
